import numpy as np, ml_dtypes
CORES = [100,101,102,103,108,109,110,111]
N = 8
TK = 512
def setup_inputs(rng):
    return {"b": rng.standard_normal((N, 128, TK), dtype=np.float32).astype(ml_dtypes.bfloat16), "l": (rng.standard_normal((N, 128, N * 128), dtype=np.float32) / 16).astype(ml_dtypes.bfloat16)}
def setup_inputs_big(rng):
    d = setup_inputs(rng)
    for k in ("b",): d[k] = (d[k].astype(np.float32) * 1048576.0).astype(d[k].dtype)
    return d
def setup_inputs_small(rng):
    d = setup_inputs(rng)
    for k in ("b",): d[k] = (d[k].astype(np.float32) * (1 / 1048576.0)).astype(d[k].dtype)
    return d
def setup_inputs_apart(rng):
    d = setup_inputs(rng)
    f = (10.0 ** rng.permutation(np.linspace(-1.5, 1.5, N))).astype(np.float32).reshape(N, 1, 1)
    for k in ("b",): d[k] = (d[k].astype(np.float32) * f).astype(d[k].dtype)
    return d
def reference(b, l):
    B, L = b.astype(np.float64), l.astype(np.float64)
    y = np.zeros((N, 128, TK))
    for r in range(N):
        acc = B[r].copy()
        for s in range(r):
            acc -= L[r][:, 128 * s:128 * s + 128].T @ y[s]
        y[r] = acc
    return {"y": y.astype(ml_dtypes.bfloat16)}

@@ -1,0 +1,244 @@
+import comms_topo
+from concourse.bass import DstId, RemoteDMATransfer
+from concourse.mybir import AluOpType
+
+N, TK, TB = 8, 512, 128
+CORES = [100, 101, 102, 103, 108, 109, 110, 111]
+NA = sum(1 for c in CORES if comms_topo.chip(c) == comms_topo.chip(CORES[0]))
+NB = N - NA
+CW = TK // NB
+HW = TK // 2
+NP = max((HW // CW) * (NA - 1), NB)
+BF = "bfloat16"
+
+SCRATCH = {
+    "S": ("sbuf", [128, TK + TB * (NA - 1)], BF),
+    "G": ("sbuf", [128, (HW // CW) * (NA - 1) * CW], BF),
+    "OUT": ("sbuf", [128, TK], BF),
+    "BFULL": ("sbuf", [128, TK], BF),
+    "BS": ("sbuf", [128, NB * CW], BF),
+    "Y0": ("sbuf", [128, CW], BF),
+    "YA": ("sbuf", [128, (NA - 1) * CW], BF),
+    "RB": ("sbuf", [128, NB * CW], BF),
+}
+for _s in range(NA):
+    SCRATCH["R%d" % _s] = ("sbuf", [128, HW + TB * _s], BF)
+for _r in range(NA, N):
+    SCRATCH["L%d" % _r] = ("sbuf", [128, TB * _r], BF)
+for _p in range(NP):
+    SCRATCH["P%d" % _p] = ("psum", [128, 512], "float32")
+
+SEMAPHORES = (["ld", "st", "snt", "x0", "x1", "pre", "fin"] + ["ra%d" % s for s in range(NA)]
+              + ["m%d" % p for p in range(NP)] + ["v%d" % p for p in range(NP)])
+
+
+def rank_program(g, core, T, topo):
+    rank = T.rank_of(core)
+    if rank is None:
+        return
+    cores = list(T.cores)
+    A, B = cores[:NA], cores[NA:]
+    GW = [c for c in A if all(topo.may_write(c, d) for d in B)]
+    Q = NB // len(GW)
+    sem = T.sem
+    sent = [0]
+
+    def count(src, dst):
+        return bin(topo.mask(src, dst)).count("1")
+
+    def pick(dst, lo, n):
+        m = topo.mask(core, dst)
+        es = [e for e in range(m.bit_length()) if (m >> e) & 1]
+        return sum(1 << e for e in es[lo:lo + n])
+
+    def did(c):
+        rid, pid, _ = topo.addr(c)
+        return DstId(rid=rid, pnc=pid)
+
+    def send(items):
+        trs = []
+        for d, dap, sap, m, sn in items:
+            trs.append(RemoteDMATransfer(dst_ids=[did(d)], dma_engine_mask=m, remote_sem=sem[sn], src=sap, dst=dap))
+            sent[0] += bin(m).count("1")
+        g.remote_dma_fused(trs, local_sem=sem.snt)
+
+    def waiter(q):
+        seen = {}
+
+        def need(name, val):
+            if seen.get(name, 0) < val:
+                q.wait_ge(sem[name], val)
+                seen[name] = val
+        return need
+
+    gn, tn, vn, sn_ = waiter(g), waiter(g.tensor), waiter(g.vector), waiter(g.sync)
+
+    def P(i):
+        return T["P%d" % i][:, 0:CW]
+
+    e_on = count(A[0], A[1])
+    e_off = count(GW[0], B[0])
+    ne1 = e_on // len(GW)
+    nx = e_off // Q
+    npost = e_on // (Q * (NA - 2))
+    nbs = 4
+
+    def plan(k):
+        calls = []
+        for grp in (range(0, NB // 2), range(NB // 2, NB)):
+            rows = [i for i in grp if i != k]
+            ne = e_on // len(rows)
+            calls.append([(i, n * ne, ne) for n, i in enumerate(rows)])
+        return calls
+
+    if core in A:
+        s = rank
+        wt = TB * s
+        if s == 0:
+            g.sync.dma_start(T.S[:, 0:TK], T.b[:, :]).then_inc(sem.ld, 16)
+            g.scalar.dma_start(T.y[:, :], T.b[:, :]).then_inc(sem.st, 16)
+            g.scalar.wait_ge(sem.st, 16)
+            nld = 1
+        else:
+            g.sync.dma_start(T.S[:, 0:HW], T.b[:, 0:HW]).then_inc(sem.ld, 16)
+            g.scalar.dma_start(T.S[:, HW:HW + wt], T.l[:, 0:wt]).then_inc(sem.ld, 16)
+            g.sync.dma_start(T.S[:, HW + wt:TK + wt], T.b[:, HW:TK]).then_inc(sem.ld, 16)
+            nld = 3
+        gn("ld", 16 * nld)
+        items = []
+        for j, gw in enumerate(GW):
+            if gw != core:
+                items.append((gw, T["R%d" % s][:, :], T.S[:, j * HW:j * HW + HW + wt],
+                              pick(gw, len(items) * ne1, ne1), "ra%d" % s))
+        send(items)
+
+        if core in GW:
+            j = GW.index(core)
+
+            def src_of(t):
+                if t == s:
+                    return T.S, j * (HW + TB * t), HW, ("ld", 16 * nld)
+                return T["R%d" % t], (0 if j == 0 else TB * t), (HW if j == 0 else 0), ("ra%d" % t, ne1)
+
+            def bsl(t, q):
+                buf, bo, _, _ = src_of(t)
+                return buf[:, bo + q * CW:bo + (q + 1) * CW]
+
+            def tile(r, t):
+                buf, _, to, _ = src_of(r)
+                return buf[:, to + t * TB:to + (t + 1) * TB]
+
+            def ysl(t, q):
+                if t == 0:
+                    return bsl(0, q)
+                o = (q * (NA - 1) + t - 1) * CW
+                return T.G[:, o:o + CW]
+
+            def idx(t, q):
+                return (t - 1) * Q + q
+
+            for r in range(1, NA):
+                tn(*src_of(r)[3])
+                for t in range(r):
+                    for q in range(Q):
+                        if t == 0:
+                            tn(*src_of(0)[3])
+                        else:
+                            tn("v%d" % idx(t, q), 1)
+                        mm = g.tensor.matmul(P(idx(r, q)), tile(r, t), ysl(t, q), start=(t == 0), stop=(t == r - 1))
+                        if t == r - 1:
+                            mm.then_inc(sem["m%d" % idx(r, q)], 1)
+            for r in range(1, NA):
+                for q in range(Q):
+                    vn(*src_of(r)[3])
+                    vn("m%d" % idx(r, q), 1)
+                    g.vector.tensor_tensor(ysl(r, q), bsl(r, q), P(idx(r, q)),
+                                           AluOpType.subtract).then_inc(sem["v%d" % idx(r, q)], 1)
+            gn(*src_of(0)[3])
+            send([(B[j * Q + q], T.Y0[:, :], bsl(0, q), pick(B[j * Q + q], q * nx, nx), "x0") for q in range(Q)])
+            for r in range(1, NA):
+                for q in range(Q):
+                    gn("v%d" % idx(r, q), 1)
+            wg = (NA - 1) * CW
+            send([(B[j * Q + q], T.YA[:, :], T.G[:, q * wg:(q + 1) * wg], pick(B[j * Q + q], q * nx, nx), "x1")
+                  for q in range(Q)])
+            items = []
+            for r in range(1, NA):
+                if A[r] != core:
+                    for q in range(Q):
+                        c0 = (j * Q + q) * CW
+                        items.append((A[r], T.OUT[:, c0:c0 + CW], ysl(r, q),
+                                      pick(A[r], len(items) * npost, npost), "fin"))
+            send(items)
+            nst = 0
+            for q in range(Q):
+                c0 = (j * Q + q) * CW
+                sn_("v%d" % idx(s, q), 1)
+                g.sync.dma_start(T.y[:, c0:c0 + CW], ysl(s, q)).then_inc(sem.st, 16)
+                nst += 1
+        else:
+            nst = 0
+        if s > 0:
+            others = [jj for jj, gw in enumerate(GW) if gw != core]
+            sn_("fin", len(others) * Q * npost)
+            for jj in others:
+                g.sync.dma_start(T.y[:, jj * HW:(jj + 1) * HW], T.OUT[:, jj * HW:(jj + 1) * HW]).then_inc(sem.st, 16)
+                nst += 1
+            sn_("st", 16 * nst)
+    else:
+        k = rank - NA
+        own = T["L%d" % rank]
+        g.sync.dma_start(own[:, :], T.l[:, 0:TB * rank]).then_inc(sem.ld, 16)
+        g.scalar.dma_start(T.BFULL[:, :], T.b[:, :]).then_inc(sem.ld, 16)
+        peers = [p for p in range(NB) if p != k]
+        gn("ld", 32)
+        g.remote_dma_fused([RemoteDMATransfer(dst_ids=[did(B[p]) for p in peers],
+                                              dma_engine_mask=pick(B[peers[0]], 0, e_on), remote_sem=sem.pre,
+                                              srcs=[own[:, :]], dsts=[own[:, :] for p in peers])], local_sem=sem.snt)
+        sent[0] += e_on
+        send([(B[p], T.BS[:, k * CW:(k + 1) * CW], T.BFULL[:, p * CW:(p + 1) * CW], pick(B[p], n * nbs, nbs), "pre")
+              for n, p in enumerate(peers)])
+        pre = len(peers) * (e_on + nbs)
+
+        def tile(r, t):
+            return T["L%d" % r][:, t * TB:(t + 1) * TB]
+
+        def yv(t):
+            if t == 0:
+                return T.Y0[:, :]
+            if t < NA:
+                return T.YA[:, (t - 1) * CW:t * CW]
+            i = t - NA
+            return T.OUT[:, k * CW:(k + 1) * CW] if i == k else T.RB[:, i * CW:(i + 1) * CW]
+
+        tn("ld", 32)
+        tn("pre", pre)
+        tn("x0", nx)
+        for i in range(NB):
+            g.tensor.matmul(P(i), tile(NA + i, 0), yv(0), start=True, stop=False)
+        tn("x1", nx)
+        for i in range(NB):
+            r = NA + i
+            for t in range(1, r):
+                if t >= NA:
+                    tn("v%d" % (t - NA), 1)
+                mm = g.tensor.matmul(P(i), tile(r, t), yv(t), start=False, stop=(t == r - 1))
+                if t == r - 1:
+                    mm.then_inc(sem["m%d" % i], 1)
+        vn("ld", 32)
+        vn("pre", pre)
+        for i in range(NB):
+            vn("m%d" % i, 1)
+            bs = T.BFULL[:, k * CW:(k + 1) * CW] if i == k else T.BS[:, i * CW:(i + 1) * CW]
+            g.vector.tensor_tensor(yv(NA + i), bs, P(i), AluOpType.subtract).then_inc(sem["v%d" % i], 1)
+        for call in plan(k):
+            for i, _, _ in call:
+                gn("v%d" % i, 1)
+            send([(B[i], T.OUT[:, k * CW:(k + 1) * CW], T.RB[:, i * CW:(i + 1) * CW], pick(B[i], lo, ne), "fin")
+                  for i, lo, ne in call])
+        fin = sum(ne for kk in peers for call in plan(kk) for i, _, ne in call if i == k)
+        sn_("fin", fin)
+        sn_("v%d" % k, 1)
+        g.sync.dma_start(T.y[:, :], T.OUT[:, :]).then_inc(sem.st, 16)
+        sn_("st", 16)
+    gn("snt", sent[0])

@@ -28,7 +28,8 @@ for _r in range(NA, N):
 for _p in range(NP):
     SCRATCH["P%d" % _p] = ("psum", [128, 512], "float32")
 
-SEMAPHORES = (["ld", "st", "snt", "x0", "x1", "pre", "fin"] + ["ra%d" % s for s in range(NA)]
+SEMAPHORES = (["ld", "la", "lb", "st", "snt", "pa", "pbb", "pbt", "fin"] + ["x%d" % s for s in range(NA)]
+              + ["ra%d" % s for s in range(NA)]
               + ["m%d" % p for p in range(NP)] + ["v%d" % p for p in range(NP)])
 
 
@@ -78,10 +79,12 @@ def rank_program(g, core, T, topo):
 
     e_on = count(A[0], A[1])
     e_off = count(GW[0], B[0])
-    ne1 = e_on // len(GW)
     nx = e_off // Q
     npost = e_on // (Q * (NA - 2))
     nbs = 4
+
+    def n1(c):
+        return e_on // len([gw for gw in GW if gw != c])
 
     def plan(k):
         calls = []
@@ -96,7 +99,8 @@ def rank_program(g, core, T, topo):
         wt = TB * s
         if s == 0:
             g.sync.dma_start(T.S[:, 0:TK], T.b[:, :]).then_inc(sem.ld, 16)
-            g.scalar.dma_start(T.y[:, :], T.b[:, :]).then_inc(sem.st, 16)
+            g.scalar.wait_ge(sem.ld, 16)
+            g.scalar.dma_start(T.y[:, :], T.S[:, 0:TK]).then_inc(sem.st, 16)
             g.scalar.wait_ge(sem.st, 16)
             nld = 1
         else:
@@ -109,7 +113,7 @@ def rank_program(g, core, T, topo):
         for j, gw in enumerate(GW):
             if gw != core:
                 items.append((gw, T["R%d" % s][:, :], T.S[:, j * HW:j * HW + HW + wt],
-                              pick(gw, len(items) * ne1, ne1), "ra%d" % s))
+                              pick(gw, len(items) * n1(core), n1(core)), "ra%d" % s))
         send(items)
 
         if core in GW:
@@ -118,7 +122,7 @@ def rank_program(g, core, T, topo):
             def src_of(t):
                 if t == s:
                     return T.S, j * (HW + TB * t), HW, ("ld", 16 * nld)
-                return T["R%d" % t], (0 if j == 0 else TB * t), (HW if j == 0 else 0), ("ra%d" % t, ne1)
+                return T["R%d" % t], (0 if j == 0 else TB * t), (HW if j == 0 else 0), ("ra%d" % t, n1(A[t]))
 
             def bsl(t, q):
                 buf, bo, _, _ = src_of(t)
@@ -156,12 +160,11 @@ def rank_program(g, core, T, topo):
                                            AluOpType.subtract).then_inc(sem["v%d" % idx(r, q)], 1)
             gn(*src_of(0)[3])
             send([(B[j * Q + q], T.Y0[:, :], bsl(0, q), pick(B[j * Q + q], q * nx, nx), "x0") for q in range(Q)])
-            for r in range(1, NA):
+            for t in range(1, NA):
                 for q in range(Q):
-                    gn("v%d" % idx(r, q), 1)
-            wg = (NA - 1) * CW
-            send([(B[j * Q + q], T.YA[:, :], T.G[:, q * wg:(q + 1) * wg], pick(B[j * Q + q], q * nx, nx), "x1")
-                  for q in range(Q)])
+                    gn("v%d" % idx(t, q), 1)
+                send([(B[j * Q + q], T.YA[:, (t - 1) * CW:t * CW], ysl(t, q), pick(B[j * Q + q], q * nx, nx),
+                       "x%d" % t) for q in range(Q)])
             items = []
             for r in range(1, NA):
                 if A[r] != core:
@@ -188,17 +191,34 @@ def rank_program(g, core, T, topo):
     else:
         k = rank - NA
         own = T["L%d" % rank]
-        g.sync.dma_start(own[:, :], T.l[:, 0:TB * rank]).then_inc(sem.ld, 16)
-        g.scalar.dma_start(T.BFULL[:, :], T.b[:, :]).then_inc(sem.ld, 16)
+        wa = TB * NA
         peers = [p for p in range(NB) if p != k]
-        gn("ld", 32)
-        g.remote_dma_fused([RemoteDMATransfer(dst_ids=[did(B[p]) for p in peers],
-                                              dma_engine_mask=pick(B[peers[0]], 0, e_on), remote_sem=sem.pre,
-                                              srcs=[own[:, :]], dsts=[own[:, :] for p in peers])], local_sem=sem.snt)
-        sent[0] += e_on
-        send([(B[p], T.BS[:, k * CW:(k + 1) * CW], T.BFULL[:, p * CW:(p + 1) * CW], pick(B[p], n * nbs, nbs), "pre")
+        g.sync.dma_start(own[:, 0:wa], T.l[:, 0:wa]).then_inc(sem.la, 16)
+        g.scalar.wait_ge(sem.la, 16)
+        g.scalar.dma_start(T.BFULL[:, :], T.b[:, :]).then_inc(sem.lb, 16)
+        nlb = 16
+        if k > 0:
+            sn_("la", 16)
+            g.sync.dma_start(own[:, wa:TB * rank], T.l[:, wa:TB * rank]).then_inc(sem.lb, 16)
+            nlb += 16
+
+        def cast(lo, hi, sn):
+            g.remote_dma_fused([RemoteDMATransfer(dst_ids=[did(B[p]) for p in peers],
+                                                  dma_engine_mask=pick(B[peers[0]], 0, e_on), remote_sem=sem[sn],
+                                                  srcs=[own[:, lo:hi]], dsts=[own[:, lo:hi] for p in peers])],
+                               local_sem=sem.snt)
+            sent[0] += e_on
+
+        gn("la", 16)
+        cast(0, wa, "pa")
+        gn("lb", nlb)
+        send([(B[p], T.BS[:, k * CW:(k + 1) * CW], T.BFULL[:, p * CW:(p + 1) * CW], pick(B[p], n * nbs, nbs), "pbb")
               for n, p in enumerate(peers)])
-        pre = len(peers) * (e_on + nbs)
+        if k > 0:
+            cast(wa, TB * rank, "pbt")
+        npa = len(peers) * e_on
+        npbb = len(peers) * nbs
+        npbt = len([p for p in peers if p > 0]) * e_on
 
         def tile(r, t):
             return T["L%d" % r][:, t * TB:(t + 1) * TB]
@@ -211,22 +231,22 @@ def rank_program(g, core, T, topo):
             i = t - NA
             return T.OUT[:, k * CW:(k + 1) * CW] if i == k else T.RB[:, i * CW:(i + 1) * CW]
 
-        tn("ld", 32)
-        tn("pre", pre)
-        tn("x0", nx)
-        for i in range(NB):
-            g.tensor.matmul(P(i), tile(NA + i, 0), yv(0), start=True, stop=False)
-        tn("x1", nx)
-        for i in range(NB):
-            r = NA + i
-            for t in range(1, r):
-                if t >= NA:
-                    tn("v%d" % (t - NA), 1)
-                mm = g.tensor.matmul(P(i), tile(r, t), yv(t), start=False, stop=(t == r - 1))
+        tn("la", 16)
+        tn("pa", npa)
+        for t in range(N - 1):
+            if t < NA:
+                tn("x%d" % t, nx)
+            else:
+                tn("lb", nlb)
+                tn("pbt", npbt)
+                tn("v%d" % (t - NA), 1)
+            for i in range(max(0, t + 1 - NA), NB):
+                r = NA + i
+                mm = g.tensor.matmul(P(i), tile(r, t), yv(t), start=(t == 0), stop=(t == r - 1))
                 if t == r - 1:
                     mm.then_inc(sem["m%d" % i], 1)
-        vn("ld", 32)
-        vn("pre", pre)
+        vn("lb", nlb)
+        vn("pbb", npbb)
         for i in range(NB):
             vn("m%d" % i, 1)
             bs = T.BFULL[:, k * CW:(k + 1) * CW] if i == k else T.BS[:, i * CW:(i + 1) * CW]

import comms_topo
from concourse.bass import DstId, RemoteDMATransfer
from concourse.mybir import AluOpType

N, TK, TB = 8, 512, 128
CORES = [100, 101, 102, 103, 108, 109, 110, 111]
NA = sum(1 for c in CORES if comms_topo.chip(c) == comms_topo.chip(CORES[0]))
NB = N - NA
CW = TK // NB
HW = TK // 2
NP = max((HW // CW) * (NA - 1), NB)
BF = "bfloat16"

SCRATCH = {
    "S": ("sbuf", [128, TK + TB * (NA - 1)], BF),
    "G": ("sbuf", [128, (HW // CW) * (NA - 1) * CW], BF),
    "OUT": ("sbuf", [128, TK], BF),
    "BFULL": ("sbuf", [128, TK], BF),
    "BS": ("sbuf", [128, NB * CW], BF),
    "Y0": ("sbuf", [128, CW], BF),
    "YA": ("sbuf", [128, (NA - 1) * CW], BF),
    "RB": ("sbuf", [128, NB * CW], BF),
}
for _s in range(NA):
    SCRATCH["R%d" % _s] = ("sbuf", [128, HW + TB * _s], BF)
for _r in range(NA, N):
    SCRATCH["L%d" % _r] = ("sbuf", [128, TB * _r], BF)
for _p in range(NP):
    SCRATCH["P%d" % _p] = ("psum", [128, 512], "float32")

SEMAPHORES = (["ld", "la", "lb", "st", "snt", "pa", "pbb", "pbt", "fin"] + ["x%d" % s for s in range(NA)]
              + ["ra%d" % s for s in range(NA)]
              + ["m%d" % p for p in range(NP)] + ["v%d" % p for p in range(NP)])


def rank_program(g, core, T, topo):
    rank = T.rank_of(core)
    if rank is None:
        return
    cores = list(T.cores)
    A, B = cores[:NA], cores[NA:]
    GW = [c for c in A if all(topo.may_write(c, d) for d in B)]
    Q = NB // len(GW)
    sem = T.sem
    sent = [0]

    def count(src, dst):
        return bin(topo.mask(src, dst)).count("1")

    def pick(dst, lo, n):
        m = topo.mask(core, dst)
        es = [e for e in range(m.bit_length()) if (m >> e) & 1]
        return sum(1 << e for e in es[lo:lo + n])

    def did(c):
        rid, pid, _ = topo.addr(c)
        return DstId(rid=rid, pnc=pid)

    def send(items):
        trs = []
        for d, dap, sap, m, sn in items:
            trs.append(RemoteDMATransfer(dst_ids=[did(d)], dma_engine_mask=m, remote_sem=sem[sn], src=sap, dst=dap))
            sent[0] += bin(m).count("1")
        g.remote_dma_fused(trs, local_sem=sem.snt)

    def waiter(q):
        seen = {}

        def need(name, val):
            if seen.get(name, 0) < val:
                q.wait_ge(sem[name], val)
                seen[name] = val
        return need

    gn, tn, vn, sn_ = waiter(g), waiter(g.tensor), waiter(g.vector), waiter(g.sync)

    def P(i):
        return T["P%d" % i][:, 0:CW]

    e_on = count(A[0], A[1])
    e_off = count(GW[0], B[0])
    nx = e_off // Q
    npost = e_on // (Q * (NA - 2))
    nbs = 4

    def n1(c):
        return e_on // len([gw for gw in GW if gw != c])

    def plan(k):
        calls = []
        for grp in (range(0, NB // 2), range(NB // 2, NB)):
            rows = [i for i in grp if i != k]
            ne = e_on // len(rows)
            calls.append([(i, n * ne, ne) for n, i in enumerate(rows)])
        return calls

    if core in A:
        s = rank
        wt = TB * s
        if s == 0:
            g.sync.dma_start(T.S[:, 0:TK], T.b[:, :]).then_inc(sem.ld, 16)
            g.scalar.wait_ge(sem.ld, 16)
            g.scalar.dma_start(T.y[:, :], T.S[:, 0:TK]).then_inc(sem.st, 16)
            g.scalar.wait_ge(sem.st, 16)
            nld = 1
        else:
            g.sync.dma_start(T.S[:, 0:HW], T.b[:, 0:HW]).then_inc(sem.ld, 16)
            g.scalar.dma_start(T.S[:, HW:HW + wt], T.l[:, 0:wt]).then_inc(sem.ld, 16)
            g.sync.dma_start(T.S[:, HW + wt:TK + wt], T.b[:, HW:TK]).then_inc(sem.ld, 16)
            nld = 3
        gn("ld", 16 * nld)
        items = []
        for j, gw in enumerate(GW):
            if gw != core:
                items.append((gw, T["R%d" % s][:, :], T.S[:, j * HW:j * HW + HW + wt],
                              pick(gw, len(items) * n1(core), n1(core)), "ra%d" % s))
        send(items)

        if core in GW:
            j = GW.index(core)

            def src_of(t):
                if t == s:
                    return T.S, j * (HW + TB * t), HW, ("ld", 16 * nld)
                return T["R%d" % t], (0 if j == 0 else TB * t), (HW if j == 0 else 0), ("ra%d" % t, n1(A[t]))

            def bsl(t, q):
                buf, bo, _, _ = src_of(t)
                return buf[:, bo + q * CW:bo + (q + 1) * CW]

            def tile(r, t):
                buf, _, to, _ = src_of(r)
                return buf[:, to + t * TB:to + (t + 1) * TB]

            def ysl(t, q):
                if t == 0:
                    return bsl(0, q)
                o = (q * (NA - 1) + t - 1) * CW
                return T.G[:, o:o + CW]

            def idx(t, q):
                return (t - 1) * Q + q

            for r in range(1, NA):
                tn(*src_of(r)[3])
                for t in range(r):
                    for q in range(Q):
                        if t == 0:
                            tn(*src_of(0)[3])
                        else:
                            tn("v%d" % idx(t, q), 1)
                        mm = g.tensor.matmul(P(idx(r, q)), tile(r, t), ysl(t, q), start=(t == 0), stop=(t == r - 1))
                        if t == r - 1:
                            mm.then_inc(sem["m%d" % idx(r, q)], 1)
            for r in range(1, NA):
                for q in range(Q):
                    vn(*src_of(r)[3])
                    vn("m%d" % idx(r, q), 1)
                    g.vector.tensor_tensor(ysl(r, q), bsl(r, q), P(idx(r, q)),
                                           AluOpType.subtract).then_inc(sem["v%d" % idx(r, q)], 1)
            gn(*src_of(0)[3])
            send([(B[j * Q + q], T.Y0[:, :], bsl(0, q), pick(B[j * Q + q], q * nx, nx), "x0") for q in range(Q)])
            for t in range(1, NA):
                for q in range(Q):
                    gn("v%d" % idx(t, q), 1)
                send([(B[j * Q + q], T.YA[:, (t - 1) * CW:t * CW], ysl(t, q), pick(B[j * Q + q], q * nx, nx),
                       "x%d" % t) for q in range(Q)])
            items = []
            for r in range(1, NA):
                if A[r] != core:
                    for q in range(Q):
                        c0 = (j * Q + q) * CW
                        items.append((A[r], T.OUT[:, c0:c0 + CW], ysl(r, q),
                                      pick(A[r], len(items) * npost, npost), "fin"))
            send(items)
            nst = 0
            for q in range(Q):
                c0 = (j * Q + q) * CW
                sn_("v%d" % idx(s, q), 1)
                g.sync.dma_start(T.y[:, c0:c0 + CW], ysl(s, q)).then_inc(sem.st, 16)
                nst += 1
        else:
            nst = 0
        if s > 0:
            others = [jj for jj, gw in enumerate(GW) if gw != core]
            sn_("fin", len(others) * Q * npost)
            for jj in others:
                g.sync.dma_start(T.y[:, jj * HW:(jj + 1) * HW], T.OUT[:, jj * HW:(jj + 1) * HW]).then_inc(sem.st, 16)
                nst += 1
            sn_("st", 16 * nst)
    else:
        k = rank - NA
        own = T["L%d" % rank]
        wa = TB * NA
        peers = [p for p in range(NB) if p != k]
        g.sync.dma_start(own[:, 0:wa], T.l[:, 0:wa]).then_inc(sem.la, 16)
        g.scalar.wait_ge(sem.la, 16)
        g.scalar.dma_start(T.BFULL[:, :], T.b[:, :]).then_inc(sem.lb, 16)
        nlb = 16
        if k > 0:
            sn_("la", 16)
            g.sync.dma_start(own[:, wa:TB * rank], T.l[:, wa:TB * rank]).then_inc(sem.lb, 16)
            nlb += 16

        def cast(lo, hi, sn):
            g.remote_dma_fused([RemoteDMATransfer(dst_ids=[did(B[p]) for p in peers],
                                                  dma_engine_mask=pick(B[peers[0]], 0, e_on), remote_sem=sem[sn],
                                                  srcs=[own[:, lo:hi]], dsts=[own[:, lo:hi] for p in peers])],
                               local_sem=sem.snt)
            sent[0] += e_on

        gn("la", 16)
        cast(0, wa, "pa")
        gn("lb", nlb)
        send([(B[p], T.BS[:, k * CW:(k + 1) * CW], T.BFULL[:, p * CW:(p + 1) * CW], pick(B[p], n * nbs, nbs), "pbb")
              for n, p in enumerate(peers)])
        if k > 0:
            cast(wa, TB * rank, "pbt")
        npa = len(peers) * e_on
        npbb = len(peers) * nbs
        npbt = len([p for p in peers if p > 0]) * e_on

        def tile(r, t):
            return T["L%d" % r][:, t * TB:(t + 1) * TB]

        def yv(t):
            if t == 0:
                return T.Y0[:, :]
            if t < NA:
                return T.YA[:, (t - 1) * CW:t * CW]
            i = t - NA
            return T.OUT[:, k * CW:(k + 1) * CW] if i == k else T.RB[:, i * CW:(i + 1) * CW]

        tn("la", 16)
        tn("pa", npa)
        for t in range(N - 1):
            if t < NA:
                tn("x%d" % t, nx)
            else:
                tn("lb", nlb)
                tn("pbt", npbt)
                tn("v%d" % (t - NA), 1)
            for i in range(max(0, t + 1 - NA), NB):
                r = NA + i
                mm = g.tensor.matmul(P(i), tile(r, t), yv(t), start=(t == 0), stop=(t == r - 1))
                if t == r - 1:
                    mm.then_inc(sem["m%d" % i], 1)
        vn("lb", nlb)
        vn("pbb", npbb)
        for i in range(NB):
            vn("m%d" % i, 1)
            bs = T.BFULL[:, k * CW:(k + 1) * CW] if i == k else T.BS[:, i * CW:(i + 1) * CW]
            g.vector.tensor_tensor(yv(NA + i), bs, P(i), AluOpType.subtract).then_inc(sem["v%d" % i], 1)
        for call in plan(k):
            for i, _, _ in call:
                gn("v%d" % i, 1)
            send([(B[i], T.OUT[:, k * CW:(k + 1) * CW], T.RB[:, i * CW:(i + 1) * CW], pick(B[i], lo, ne), "fin")
                  for i, lo, ne in call])
        fin = sum(ne for kk in peers for call in plan(kk) for i, _, ne in call if i == k)
        sn_("fin", fin)
        sn_("v%d" % k, 1)
        g.sync.dma_start(T.y[:, :], T.OUT[:, :]).then_inc(sem.st, 16)
        sn_("st", 16)
    gn("snt", sent[0])
